import numpy as np
import ml_dtypes


def mxq(x, axis, fmt="e4m3"):
    dtype, down = {"e4m3": (ml_dtypes.float8_e4m3fn, 7), "e5m2": (ml_dtypes.float8_e5m2, 14)}[fmt]
    v = np.moveaxis(np.asarray(x, np.float32).astype(ml_dtypes.bfloat16).astype(np.float64), axis, -1)
    blocks = v.reshape(v.shape[:-1] + (-1, 32))
    amax = np.abs(blocks).max(-1, keepdims=True)
    byte = np.maximum(np.where(amax > 0, np.frexp(amax)[1] - 1 + 127, 0) - down, 1)
    scale = np.exp2(byte - 127.0)
    codes = (blocks / scale).astype(np.float32).astype(dtype).astype(np.float64)
    return np.moveaxis((codes * scale).reshape(v.shape), -1, axis)


WIDE = False


def mx_kscale(k):
    if not WIDE:
        return np.ones(k)
    levels = np.array([10, -10, 5, -5, 0])
    if k % 512:
        return np.exp2(np.random.permutation(np.resize(levels, k // 32))).repeat(32)
    a = np.empty((k // 512, 16))
    for p in range(k // 512):
        a[p, :8] = np.random.permutation(np.resize(levels, 8))
        for g in range(8):
            far = levels[np.abs(levels - a[p, g]) >= 10]
            a[p, g + 8] = far[np.random.randint(len(far))]
    return np.exp2(a.ravel()).repeat(32)


BF16 = ml_dtypes.bfloat16


def bf(x):
    return np.asarray(x, np.float32).astype(BF16)


def f64(x):
    return np.asarray(x).astype(np.float64)


E2M1 = np.array([0.0, 0.5, 1.0, 1.5, 2.0, 3.0, 4.0, 6.0, -0.0, -0.5, -1.0, -1.5, -2.0, -3.0, -4.0, -6.0])


def pack_weight(w, fmt):
    k, n = w.shape
    w = f64(bf(w)).reshape(k // 32, 32, n)
    amax = np.abs(w).max(1)
    if fmt == "e4m3":
        byte = np.frexp(amax)[1] - 1 + 127 - 7
    else:
        mant, ex = np.frexp(amax / 6.0)
        byte = np.where(mant > 0.5, ex, ex - 1) + 127
    byte = np.clip(np.where(amax > 0, byte, 1), 1, 254)
    scaled = (w * np.exp2(127.0 - byte)[:, None, :]).reshape(k, n).astype(np.float32)
    by_word = np.ascontiguousarray(scaled.reshape(k // 512, 128, 4, n).transpose(0, 1, 3, 2))
    if fmt == "e4m3":
        words = by_word.astype(ml_dtypes.float8_e4m3fn).view(np.uint8)
    else:
        c = by_word.astype(ml_dtypes.float4_e2m1fn).view(np.uint8) & 0xF
        words = c[..., 0::2] | (c[..., 1::2] << 4)
    return np.ascontiguousarray(words), np.ascontiguousarray(byte.astype(np.uint8).reshape(k // 512, 16, n))


def unpack_weight(words, scales, fmt):
    g, p, n, _ = words.shape
    if fmt == "e4m3":
        vals = np.ascontiguousarray(words).view(ml_dtypes.float8_e4m3fn).astype(np.float64)
    else:
        nib = np.empty((g, p, n, 4), np.uint8)
        nib[..., 0::2] = words & 0xF
        nib[..., 1::2] = words >> 4
        vals = E2M1[nib]
    vals = vals * np.repeat(np.exp2(scales.astype(np.float64) - 127.0), 8, axis=1)[..., None]
    return vals.transpose(0, 1, 3, 2).reshape(g * 512, n)
def pack4(w):
    words, scales = pack_weight(w, "e2m1")
    return words.reshape(words.shape[0], 128, -1), scales


def unpack4(words, scales):
    return unpack_weight(words.reshape(words.shape[0], 128, -1, 2), scales, "e2m1")


def planes(Y):
    n, m = Y.shape
    b = f64(bf(Y)).reshape(n // 32, 32, m)
    amax = np.abs(b).max(1)
    byte = np.clip(np.where(amax > 0, np.frexp(amax)[1] - 1 + 127 - 7, 1), 1, 254)
    codes = (b * np.exp2(127.0 - byte)[:, None, :]).reshape(n, m).astype(np.float32).astype(ml_dtypes.float8_e4m3fn).view(np.uint8)
    words = codes.reshape(n // 512, 128, 4, m).transpose(0, 1, 3, 2)
    return np.ascontiguousarray(words), np.ascontiguousarray(byte.astype(np.uint8).reshape(n // 512, 16, m))


T, DI, DO = 1536, 1024, 1024

CLIP_A = 2.0
RANGE_W = 1.6
ERR = 0.6


def noise(*shape):
    return np.random.standard_normal(shape)


def setup_inputs():
    s = mx_kscale(T)[:, None]
    a = np.clip(noise(T, DI), -CLIP_A, CLIP_A) * np.exp(0.8 * noise(DI))
    a_words, a_scales = pack_weight(a * s, "e4m3")
    err4_words, err4_scales = pack4(ERR * noise(T, DO) / np.sqrt(T) / s)
    err8_words, err8_scales = pack_weight(ERR * noise(T, DO) / np.sqrt(T) / s, "e4m3")
    err = bf(ERR * noise(T, DO) / np.sqrt(T) / s)
    w_mag = bf(np.abs(noise(DI, DO)))
    w_range = bf(RANGE_W * np.exp(0.1 * noise(DO)))
    return {"a_words": a_words, "a_scales": a_scales,
            "err4_words": err4_words, "err4_scales": err4_scales,
            "err8_words": err8_words, "err8_scales": err8_scales,
            "err": err, "w_mag": w_mag, "w_range": w_range}


def reference(a_words, a_scales, err4_words, err4_scales, err8_words, err8_scales, err, w_mag, w_range):
    A = unpack_weight(a_words, a_scales, "e4m3")
    P = unpack4(err4_words, err4_scales)
    Q = unpack_weight(err8_words, err8_scales, "e4m3")
    R = mxq(f64(err), 0, "e4m3")
    grad = (A.T @ P) + (A.T @ Q) + (A.T @ R)
    y = grad * (f64(w_mag) <= f64(w_range))
    Y = y
    words, scales = planes(Y)
    return y, words, scales

@@ -1,0 +1,305 @@
+from contextlib import ExitStack
+
+import concourse.mybir as mybir
+
+T, DI, DO = 1536, 1024, 1024
+FLOPS = 3 * 2 * T * DI * DO
+
+F32 = mybir.dt.float32
+BF16 = mybir.dt.bfloat16
+I32 = mybir.dt.int32
+U32 = mybir.dt.uint32
+U8 = mybir.dt.uint8
+FP8X4 = mybir.dt.float8_e4m3fn_x4
+FP4X4 = mybir.dt.float4_e2m1fn_x4
+ALU = mybir.AluOpType
+
+P = 128
+PACK = 4
+GROUP = P * PACK
+G = T // GROUP
+HALF = 512
+Q_ROW = 4
+LAST_CHUNKS = (256, 128, 128)
+
+
+def tile_straight_through_weight_grad_k3_kernel(
+    tc, a_words, a_scales, err4_words, err4_scales, err8_words, err8_scales, err, w_mag, w_range, out_0, out_1, out_2
+):
+    nc = tc.nc
+    with ExitStack() as ctx:
+        keep = ctx.enter_context(tc.tile_pool(name="keep", bufs=1))
+        stage = ctx.enter_context(tc.tile_pool(name="stage", bufs=3))
+        psum = ctx.enter_context(tc.psum_pool(name="psum", bufs=1))
+        ctx.enter_context(tc.manual_schedule())
+
+        def kept(name, shape, dtype):
+            return keep.tile(shape, dtype, name=name, align_bytes=64)
+
+        a_raw = [kept("a_raw%d" % g, [P, DI], U32) for g in range(G)]
+        a_codes = [[kept("a_codes%d%d" % (g, m), [P, HALF], U32) for m in range(2)] for g in range(G)]
+        a_sc_raw = kept("a_sc_raw", [P, G, DI], U8)
+        a_sc = [[kept("a_sc%d%d" % (g, m), [P, HALF], U8) for m in range(2)] for g in range(G)]
+        q_codes = [kept("q_codes%d" % h, [P, G, HALF], U32) for h in range(2)]
+        q_sc = kept("q_sc", [P, G, DO], U8)
+        p_codes = [kept("p_codes%d" % h, [P, G, 2 * HALF], U8) for h in range(2)]
+        p_sc = kept("p_sc", [P, G, DO], U8)
+        r_raw = [[kept("r_raw%d%d" % (g, h), [P, PACK, HALF], BF16) for h in range(2)] for g in range(G)]
+        r_codes = [[kept("r_codes%d%d" % (g, h), [P, HALF], U32) for h in range(2)] for g in range(G)]
+        r_sc = [[kept("r_sc%d%d" % (g, h), [P, HALF], U8) for h in range(2)] for g in range(G)]
+        mag = [[kept("mag%d%d" % (m, h), [P, PACK, HALF], BF16) for h in range(2)] for m in range(2)]
+        mask = [[kept("mask%d%d" % (m, h), [P, PACK, HALF], BF16) for h in range(2)] for m in range(2)]
+        y = [[kept("y%d%d" % (m, h), [P, PACK, HALF], F32) for h in range(2)] for m in range(2)]
+        y_codes = [[kept("y_codes%d%d" % (m, h), [P, HALF], U32) for h in range(2)] for m in range(2)]
+        y_sc = kept("y_sc", [P, 2, DO], U8)
+        range_rows = kept("range_rows", [P, 32], BF16)
+        range_cols = kept("range_cols", [P, 32], BF16)
+        range_wide = kept("range_wide", [P, 32, 32], BF16)
+        range_all = kept("range_all", [P, DO], BF16)
+
+        def half(h):
+            return slice(h * HALF, (h + 1) * HALF)
+
+        def words_of(dram, g):
+            return dram[g].rearrange("p n t -> p (n t)").bitcast(I32)
+
+        def load_a(g, cols):
+            nc.sync.dma_start(out=a_raw[g][:, cols].bitcast(I32), in_=words_of(a_words, g)[:, cols])
+
+        def load_q(g, h):
+            nc.sync.dma_start(out=q_codes[h][:, g, :].bitcast(I32), in_=words_of(err8_words, g)[:, half(h)])
+
+        def load_q_all(h):
+            src = err8_words.rearrange("g p n t -> p g (n t)").bitcast(I32)
+            nc.sync.dma_start(out=q_codes[h][:].bitcast(I32), in_=src[:, :, half(h)])
+
+        def load_p(h):
+            src = err4_words.rearrange("g p b -> p g b")[:, :, 2 * HALF * h : 2 * HALF * (h + 1)]
+            nc.sync.dma_start(out=p_codes[h][:].bitcast(I32), in_=src.bitcast(I32))
+
+        def load_scales(plane, dram, first_row):
+            src = dram.rearrange("g (q r) n -> r q g n", r=4)
+            for r in range(4):
+                nc.sync.dma_start(out=plane[first_row + r : P : 32, :, :].bitcast(I32), in_=src[r].bitcast(I32))
+
+        def load_rows(tile, dram, g, h):
+            src = dram[g * GROUP : (g + 1) * GROUP, :].rearrange("(p t) n -> p t n", t=PACK)
+            nc.sync.dma_start(out=tile[:], in_=src[:, :, half(h)])
+
+        def order_a_codes(g, m):
+            nc.vector.tensor_copy(
+                out=a_codes[g][m][:].bitcast(I32).rearrange("p (t c) -> p c t", t=PACK),
+                in_=a_raw[g][:, half(m)].bitcast(I32).rearrange("p (c t) -> p c t", t=PACK),
+            )
+
+        def order_a_scales(g, m):
+            nc.vector.tensor_copy(
+                out=a_sc[g][m][:].rearrange("p (t c) -> p t c", t=PACK),
+                in_=a_sc_raw[:, g, half(m)].rearrange("p (c t) -> p t c", t=PACK),
+            )
+
+        def interleave(copy, src, width):
+            grouped = stage.tile([P, HALF * PACK], BF16, name="grouped", align_bytes=64)
+            copy(
+                out=grouped[:, : width * PACK].rearrange("p (c i t) -> p c t i", i=4, t=PACK),
+                in_=src.rearrange("p t (c i) -> p c t i", i=4),
+            )
+            return grouped[:, : width * PACK]
+
+        def quantize_r(g, h, grouped):
+            nc.vector.quantize_mx(out=r_codes[g][h][:].bitcast(FP8X4), scales=r_sc[g][h][:], in_=grouped)
+
+        def quantize_y(m, h, cols, grouped):
+            whole = slice(h * HALF + cols.start, h * HALF + cols.stop)
+            nc.vector.quantize_mx(out=y_codes[m][h][:, cols].bitcast(FP8X4), scales=y_sc[:, m, whole], in_=grouped)
+
+        def make_mask(m, h):
+            nc.vector.tensor_tensor(
+                out=mask[m][h][:],
+                in0=mag[m][h][:],
+                in1=range_all[:, half(h)].unsqueeze(1).to_broadcast([P, PACK, HALF]),
+                op=ALU.is_le,
+            )
+
+        def apply_mask(acc, m, h, t, cols):
+            nc.vector.tensor_tensor(out=y[m][h][:, t, cols], in0=acc, in1=mask[m][h][:, t, cols], op=ALU.mult)
+
+        banks_used = []
+
+        def new_acc(width):
+            bank = len(banks_used) % 8
+            banks_used.append(bank)
+            acc = psum.tile([P, HALF], F32, name="acc%d" % bank)
+            return acc[:, :width]
+
+        def mx(acc, g, m, t, codes, scales, start=False, stop=False):
+            mine = slice(t * P, (t + 1) * P)
+            nc.tensor.matmul_mx(
+                out=acc,
+                lhsT=a_codes[g][m][:, mine].bitcast(FP8X4),
+                lhsT_scale=a_sc[g][m][:, mine],
+                rhs=codes,
+                rhs_scale=scales,
+                start=start,
+                stop=stop,
+            )
+
+        def pass_q(acc, g, m, h, t, cols):
+            whole = slice(h * HALF + cols.start, h * HALF + cols.stop)
+            mx(acc, g, m, t, q_codes[h][:, g, cols].bitcast(FP8X4), q_sc[Q_ROW:P, g, whole], start=(g == 0))
+
+        def pass_p(acc, g, m, h, t, cols):
+            width = cols.stop - cols.start
+            step = width if width == HALF else P
+            for c in range(0, width, step):
+                lo = cols.start + c
+                codes = p_codes[h][:, g, 2 * lo : 2 * (lo + step)].bitcast(FP4X4)
+                mx(acc[:, c : c + step], g, m, t, codes, p_sc[:, g, h * HALF + lo : h * HALF + lo + step])
+
+        def pass_r(acc, g, m, h, t, cols):
+            mx(acc, g, m, t, r_codes[g][h][:, cols].bitcast(FP8X4), r_sc[g][h][:, cols], stop=(g == G - 1))
+
+        def store_y(m, h, ts, cols):
+            dst = out_0[m * GROUP : (m + 1) * GROUP, :].rearrange("(p t) n -> p t n", t=PACK)
+            nc.sync.dma_start(out=dst[:, ts, h * HALF + cols.start : h * HALF + cols.stop], in_=y[m][h][:, ts, cols])
+
+        def store_codes(m, h, cols):
+            dst = out_1[m].rearrange("p n t -> p (n t)").bitcast(I32)
+            nc.sync.dma_start(
+                out=dst[:, h * HALF + cols.start : h * HALF + cols.stop], in_=y_codes[m][h][:, cols].bitcast(I32)
+            )
+
+        def store_scales(ms, h, queues):
+            dst = out_2.rearrange("m q n -> q m n")
+            for q in range(4):
+                queues[q].dma_start(
+                    out=dst[4 * q : 4 * q + 4, ms, half(h)].bitcast(I32),
+                    in_=y_sc[32 * q : 32 * q + 4, ms, half(h)].bitcast(I32),
+                )
+
+        full = slice(0, HALF)
+        all_t = slice(0, PACK)
+
+        for plane in (a_sc_raw, q_sc, p_sc):
+            nc.vector.memset(plane[:].rearrange("p g n -> p (g n)").bitcast(I32), 0)
+
+        load_a(0, half(0))
+        load_q(0, 0)
+        load_scales(a_sc_raw, a_scales, 0)
+        load_scales(q_sc, err8_scales, Q_ROW)
+        load_a(0, half(1))
+        load_a(1, slice(0, DI))
+        load_q(1, 0)
+        nc.sync.dma_start(out=range_rows[:], in_=w_range.rearrange("(b i) -> b i", i=32).partition_broadcast(4))
+        load_a(2, slice(0, DI))
+        load_q(2, 0)
+        load_rows(r_raw[0][0], err, 0, 0)
+        load_scales(p_sc, err4_scales, 0)
+        load_p(0)
+        load_rows(r_raw[1][0], err, 1, 0)
+        load_rows(r_raw[2][0], err, 2, 0)
+        load_rows(mag[0][0], w_mag, 0, 0)
+        load_rows(mag[1][0], w_mag, 1, 0)
+        load_q_all(1)
+        load_p(1)
+        for g in range(G):
+            load_rows(r_raw[g][1], err, g, 1)
+        load_rows(mag[0][1], w_mag, 0, 1)
+        load_rows(mag[1][1], w_mag, 1, 1)
+
+        order_a_codes(0, 0)
+        order_a_scales(0, 0)
+        order_a_scales(0, 1)
+        order_a_codes(0, 1)
+        for g in (1, 2):
+            order_a_scales(g, 0)
+            order_a_scales(g, 1)
+            order_a_codes(g, 0)
+            order_a_codes(g, 1)
+            if g == 1:
+                nc.vector.transpose(out=range_cols[:], in_=range_rows[:])
+                nc.scalar.copy(out=range_wide[:], in_=range_cols[:].unsqueeze(2).to_broadcast([P, 32, 32]))
+        nc.vector.transpose(out=range_all[:], in_=range_wide[:].rearrange("p b j -> p (b j)"))
+
+        acc = [[new_acc(HALF) for t in range(PACK)] for m in range(2)]
+        for one_pass in (pass_q, pass_p):
+            for g in range(G):
+                for m in range(2):
+                    for t in range(PACK):
+                        one_pass(acc[m][t], g, m, 0, t, full)
+
+        grouped = [interleave(nc.scalar.copy, r_raw[g][0][:], HALF) for g in range(G)]
+        quantize_r(0, 0, grouped[0])
+        quantize_r(1, 0, grouped[1])
+        make_mask(0, 0)
+        quantize_r(2, 0, grouped[2])
+        make_mask(1, 0)
+
+        for g in range(G):
+            for t in range(PACK):
+                pass_r(acc[0][t], g, 0, 0, t, full)
+        for t in range(PACK):
+            for g in range(G):
+                pass_r(acc[1][t], g, 1, 0, t, full)
+
+        grouped = [interleave(nc.scalar.copy, r_raw[g][1][:], HALF) for g in range(G)]
+        for t in range(PACK):
+            apply_mask(acc[0][t], 0, 0, t, full)
+        store_y(0, 0, all_t, full)
+        quantize_r(0, 1, grouped[0])
+        apply_mask(acc[1][0], 1, 0, 0, full)
+        apply_mask(acc[1][1], 1, 0, 1, full)
+        quantize_r(1, 1, grouped[1])
+        apply_mask(acc[1][2], 1, 0, 2, full)
+        apply_mask(acc[1][3], 1, 0, 3, full)
+        store_y(1, 0, all_t, full)
+        quantize_r(2, 1, grouped[2])
+        make_mask(0, 1)
+
+        acc = [new_acc(HALF) for t in range(PACK)]
+        for t in range(PACK):
+            for one_pass in (pass_q, pass_p):
+                for g in range(G):
+                    one_pass(acc[t], g, 0, 1, t, full)
+        for t in range(PACK):
+            for g in range(G):
+                pass_r(acc[t], g, 0, 1, t, full)
+
+        quantize_y(0, 0, full, interleave(nc.scalar.copy, y[0][0][:], HALF))
+        store_codes(0, 0, full)
+        make_mask(1, 1)
+        quantize_y(1, 0, full, interleave(nc.scalar.copy, y[1][0][:], HALF))
+        store_codes(1, 0, full)
+        store_scales(slice(0, 2), 0, [nc.sync] * 4)
+
+        for t in range(PACK):
+            apply_mask(acc[t], 0, 1, t, full)
+        store_y(0, 1, all_t, full)
+        pending = (0, full, interleave(nc.scalar.copy, y[0][1][:], HALF))
+
+        lo = 0
+        for width in LAST_CHUNKS:
+            cols = slice(lo, lo + width)
+            lo += width
+            last = lo == HALF
+            for t in range(PACK):
+                acc = new_acc(width)
+                for one_pass in (pass_q, pass_p, pass_r):
+                    for g in range(G):
+                        one_pass(acc, g, 1, 1, t, cols)
+                if t == PACK - 2:
+                    quantize_y(pending[0], 1, pending[1], pending[2])
+                    store_codes(pending[0], 1, pending[1])
+                    if pending[0] == 0:
+                        store_scales(slice(0, 1), 1, [nc.sync] * 4)
+                apply_mask(acc, 1, 1, t, cols)
+                if last and t == PACK - 2:
+                    store_y(1, 1, slice(0, PACK - 1), cols)
+            if last:
+                store_y(1, 1, slice(PACK - 1, PACK), cols)
+                quantize_y(1, 1, cols, interleave(nc.vector.tensor_copy, y[1][1][:, :, cols], width))
+                store_codes(1, 1, cols)
+                store_scales(slice(1, 2), 1, [nc.scalar, nc.scalar, nc.sync, nc.sync])
+            else:
+                store_y(1, 1, all_t, cols)
+                pending = (1, cols, interleave(nc.scalar.copy, y[1][1][:, :, cols], width))

@@ -21,6 +21,7 @@ G = T // GROUP
 HALF = 512
 Q_ROW = 4
 LAST_CHUNKS = (256, 128, 128)
+WARM_PASSES = 18
 
 
 def tile_straight_through_weight_grad_k3_kernel(
@@ -41,9 +42,9 @@ def tile_straight_through_weight_grad_k3_kernel(
         a_sc_raw = kept("a_sc_raw", [P, G, DI], U8)
         a_sc = [[kept("a_sc%d%d" % (g, m), [P, HALF], U8) for m in range(2)] for g in range(G)]
         q_codes = [kept("q_codes%d" % h, [P, G, HALF], U32) for h in range(2)]
-        q_sc = kept("q_sc", [P, G, DO], U8)
+        q_sc = [kept("q_sc%d" % h, [P, G, HALF], U8) for h in range(2)]
         p_codes = [kept("p_codes%d" % h, [P, G, 2 * HALF], U8) for h in range(2)]
-        p_sc = kept("p_sc", [P, G, DO], U8)
+        p_sc = [kept("p_sc%d" % h, [P, G, HALF], U8) for h in range(2)]
         r_raw = [[kept("r_raw%d%d" % (g, h), [P, PACK, HALF], BF16) for h in range(2)] for g in range(G)]
         r_codes = [[kept("r_codes%d%d" % (g, h), [P, HALF], U32) for h in range(2)] for g in range(G)]
         r_sc = [[kept("r_sc%d%d" % (g, h), [P, HALF], U8) for h in range(2)] for g in range(G)]
@@ -77,10 +78,12 @@ def tile_straight_through_weight_grad_k3_kernel(
             src = err4_words.rearrange("g p b -> p g b")[:, :, 2 * HALF * h : 2 * HALF * (h + 1)]
             nc.sync.dma_start(out=p_codes[h][:].bitcast(I32), in_=src.bitcast(I32))
 
-        def load_scales(plane, dram, first_row):
+        def load_scales(plane, dram, first_row, cols, rows=range(4)):
             src = dram.rearrange("g (q r) n -> r q g n", r=4)
-            for r in range(4):
-                nc.sync.dma_start(out=plane[first_row + r : P : 32, :, :].bitcast(I32), in_=src[r].bitcast(I32))
+            for r in rows:
+                nc.sync.dma_start(
+                    out=plane[first_row + r : P : 32, :, :].bitcast(I32), in_=src[r][:, :, cols].bitcast(I32)
+                )
 
         def load_rows(tile, dram, g, h):
             src = dram[g * GROUP : (g + 1) * GROUP, :].rearrange("(p t) n -> p t n", t=PACK)
@@ -145,8 +148,7 @@ def tile_straight_through_weight_grad_k3_kernel(
             )
 
         def pass_q(acc, g, m, h, t, cols):
-            whole = slice(h * HALF + cols.start, h * HALF + cols.stop)
-            mx(acc, g, m, t, q_codes[h][:, g, cols].bitcast(FP8X4), q_sc[Q_ROW:P, g, whole], start=(g == 0))
+            mx(acc, g, m, t, q_codes[h][:, g, cols].bitcast(FP8X4), q_sc[h][Q_ROW:P, g, cols], start=(g == 0))
 
         def pass_p(acc, g, m, h, t, cols):
             width = cols.stop - cols.start
@@ -154,7 +156,7 @@ def tile_straight_through_weight_grad_k3_kernel(
             for c in range(0, width, step):
                 lo = cols.start + c
                 codes = p_codes[h][:, g, 2 * lo : 2 * (lo + step)].bitcast(FP4X4)
-                mx(acc[:, c : c + step], g, m, t, codes, p_sc[:, g, h * HALF + lo : h * HALF + lo + step])
+                mx(acc[:, c : c + step], g, m, t, codes, p_sc[h][:, g, lo : lo + step])
 
         def pass_r(acc, g, m, h, t, cols):
             mx(acc, g, m, t, r_codes[g][h][:, cols].bitcast(FP8X4), r_sc[g][h][:, cols], stop=(g == G - 1))
@@ -180,26 +182,51 @@ def tile_straight_through_weight_grad_k3_kernel(
         full = slice(0, HALF)
         all_t = slice(0, PACK)
 
-        for plane in (a_sc_raw, q_sc, p_sc):
+        def clear(plane):
             nc.vector.memset(plane[:].rearrange("p g n -> p (g n)").bitcast(I32), 0)
 
+        warm_in = kept("warm_in", [P, P * PACK], BF16)
+        warm_codes = kept("warm_codes", [P, P], U32)
+        warm_sc = kept("warm_sc", [P, P], U8)
+        clear(a_sc_raw)
+        clear(q_sc[0])
+        nc.vector.memset(warm_in[:], 1.0)
+        clear(p_sc[0])
+        nc.vector.quantize_mx(out=warm_codes[:].bitcast(FP8X4), scales=warm_sc[:], in_=warm_in[:])
+        clear(q_sc[1])
+        clear(p_sc[1])
+        warm_acc = psum.tile([P, HALF], F32, name="acc7")
+        for i in range(WARM_PASSES):
+            nc.tensor.matmul_mx(
+                out=warm_acc[:, :P],
+                lhsT=warm_codes[:].bitcast(FP8X4),
+                lhsT_scale=warm_sc[:],
+                rhs=warm_codes[:].bitcast(FP8X4),
+                rhs_scale=warm_sc[:],
+                start=True,
+                stop=True,
+            )
+
         load_a(0, half(0))
+        load_scales(a_sc_raw, a_scales, 0, slice(0, DI))
+        load_scales(q_sc[0], err8_scales, Q_ROW, half(0), range(0, 2))
         load_q(0, 0)
-        load_scales(a_sc_raw, a_scales, 0)
-        load_scales(q_sc, err8_scales, Q_ROW)
+        load_scales(q_sc[0], err8_scales, Q_ROW, half(0), range(2, 4))
         load_a(0, half(1))
+        load_scales(p_sc[0], err4_scales, 0, half(0))
+        load_p(0)
         load_a(1, slice(0, DI))
         load_q(1, 0)
         nc.sync.dma_start(out=range_rows[:], in_=w_range.rearrange("(b i) -> b i", i=32).partition_broadcast(4))
+        load_rows(r_raw[0][0], err, 0, 0)
         load_a(2, slice(0, DI))
         load_q(2, 0)
-        load_rows(r_raw[0][0], err, 0, 0)
-        load_scales(p_sc, err4_scales, 0)
-        load_p(0)
         load_rows(r_raw[1][0], err, 1, 0)
         load_rows(r_raw[2][0], err, 2, 0)
         load_rows(mag[0][0], w_mag, 0, 0)
         load_rows(mag[1][0], w_mag, 1, 0)
+        load_scales(q_sc[1], err8_scales, Q_ROW, half(1))
+        load_scales(p_sc[1], err4_scales, 0, half(1))
         load_q_all(1)
         load_p(1)
         for g in range(G):
@@ -222,8 +249,8 @@ def tile_straight_through_weight_grad_k3_kernel(
         nc.vector.transpose(out=range_all[:], in_=range_wide[:].rearrange("p b j -> p (b j)"))
 
         acc = [[new_acc(HALF) for t in range(PACK)] for m in range(2)]
-        for one_pass in (pass_q, pass_p):
-            for g in range(G):
+        for g in range(G):
+            for one_pass in (pass_q, pass_p):
                 for m in range(2):
                     for t in range(PACK):
                         one_pass(acc[m][t], g, m, 0, t, full)
@@ -282,6 +309,10 @@ def tile_straight_through_weight_grad_k3_kernel(
             cols = slice(lo, lo + width)
             lo += width
             last = lo == HALF
+            if last:
+                final = stage.tile([P, HALF * PACK], BF16, name="grouped", align_bytes=64)
+                final = final[:, : width * PACK]
+                by_t = final.rearrange("p (c t) -> p c t", t=PACK)
             for t in range(PACK):
                 acc = new_acc(width)
                 for one_pass in (pass_q, pass_p, pass_r):
@@ -292,14 +323,18 @@ def tile_straight_through_weight_grad_k3_kernel(
                     store_codes(pending[0], 1, pending[1])
                     if pending[0] == 0:
                         store_scales(slice(0, 1), 1, [nc.sync] * 4)
+                if last and t >= 2:
+                    nc.vector.tensor_tensor(out=by_t[:, :, t], in0=acc, in1=mask[1][1][:, t, cols], op=ALU.mult)
                 apply_mask(acc, 1, 1, t, cols)
+                if last and t == 1:
+                    nc.scalar.copy(out=by_t[:, :, 0:2], in_=y[1][1][:, 0:2, cols].rearrange("p t c -> p c t"))
                 if last and t == PACK - 2:
                     store_y(1, 1, slice(0, PACK - 1), cols)
             if last:
                 store_y(1, 1, slice(PACK - 1, PACK), cols)
-                quantize_y(1, 1, cols, interleave(nc.vector.tensor_copy, y[1][1][:, :, cols], width))
+                quantize_y(1, 1, cols, final)
                 store_codes(1, 1, cols)
-                store_scales(slice(1, 2), 1, [nc.scalar, nc.scalar, nc.sync, nc.sync])
+                store_scales(slice(1, 2), 1, [nc.sync] * 4)
             else:
                 store_y(1, 1, all_t, cols)
                 pending = (1, cols, interleave(nc.scalar.copy, y[1][1][:, :, cols], width))

@@ -21,7 +21,7 @@ G = T // GROUP
 HALF = 512
 Q_ROW = 4
 LAST_CHUNKS = (256, 128, 128)
-WARM_PASSES = 18
+WARM_FIRST, WARM_NEXT = 10, 4
 
 
 def tile_straight_through_weight_grad_k3_kernel(
@@ -39,7 +39,9 @@ def tile_straight_through_weight_grad_k3_kernel(
 
         a_raw = [kept("a_raw%d" % g, [P, DI], U32) for g in range(G)]
         a_codes = [[kept("a_codes%d%d" % (g, m), [P, HALF], U32) for m in range(2)] for g in range(G)]
-        a_sc_raw = kept("a_sc_raw", [P, G, DI], U8)
+        a_sc_first = kept("a_sc_first", [P, 1, DI], U8)
+        a_sc_rest = kept("a_sc_rest", [P, G - 1, DI], U8)
+        a_sc_raw = [a_sc_first[:, 0, :], a_sc_rest[:, 0, :], a_sc_rest[:, 1, :]]
         a_sc = [[kept("a_sc%d%d" % (g, m), [P, HALF], U8) for m in range(2)] for g in range(G)]
         q_codes = [kept("q_codes%d" % h, [P, G, HALF], U32) for h in range(2)]
         q_sc = [kept("q_sc%d" % h, [P, G, HALF], U8) for h in range(2)]
@@ -98,7 +100,7 @@ def tile_straight_through_weight_grad_k3_kernel(
         def order_a_scales(g, m):
             nc.vector.tensor_copy(
                 out=a_sc[g][m][:].rearrange("p (t c) -> p t c", t=PACK),
-                in_=a_sc_raw[:, g, half(m)].rearrange("p (c t) -> p t c", t=PACK),
+                in_=a_sc_raw[g][:, half(m)].rearrange("p (c t) -> p t c", t=PACK),
             )
 
         def interleave(copy, src, width):
@@ -188,27 +190,30 @@ def tile_straight_through_weight_grad_k3_kernel(
         warm_in = kept("warm_in", [P, P * PACK], BF16)
         warm_codes = kept("warm_codes", [P, P], U32)
         warm_sc = kept("warm_sc", [P, P], U8)
-        clear(a_sc_raw)
+        clear(a_sc_first)
         clear(q_sc[0])
         nc.vector.memset(warm_in[:], 1.0)
         clear(p_sc[0])
         nc.vector.quantize_mx(out=warm_codes[:].bitcast(FP8X4), scales=warm_sc[:], in_=warm_in[:])
+        clear(a_sc_rest)
         clear(q_sc[1])
         clear(p_sc[1])
         warm_acc = psum.tile([P, HALF], F32, name="acc7")
-        for i in range(WARM_PASSES):
-            nc.tensor.matmul_mx(
-                out=warm_acc[:, :P],
-                lhsT=warm_codes[:].bitcast(FP8X4),
-                lhsT_scale=warm_sc[:],
-                rhs=warm_codes[:].bitcast(FP8X4),
-                rhs_scale=warm_sc[:],
-                start=True,
-                stop=True,
-            )
+
+        def warm(count, lhs, lhs_scales, rhs):
+            for i in range(count):
+                nc.tensor.matmul_mx(
+                    out=warm_acc[:, :P],
+                    lhsT=lhs.bitcast(FP8X4),
+                    lhsT_scale=lhs_scales,
+                    rhs=rhs.bitcast(FP8X4),
+                    rhs_scale=warm_sc[:],
+                    start=True,
+                    stop=True,
+                )
 
         load_a(0, half(0))
-        load_scales(a_sc_raw, a_scales, 0, slice(0, DI))
+        load_scales(a_sc_first, a_scales[0:1], 0, slice(0, DI))
         load_scales(q_sc[0], err8_scales, Q_ROW, half(0), range(0, 2))
         load_q(0, 0)
         load_scales(q_sc[0], err8_scales, Q_ROW, half(0), range(2, 4))
@@ -216,19 +221,22 @@ def tile_straight_through_weight_grad_k3_kernel(
         load_scales(p_sc[0], err4_scales, 0, half(0))
         load_p(0)
         load_a(1, slice(0, DI))
+        load_scales(a_sc_rest, a_scales[1:G], 0, slice(0, DI))
         load_q(1, 0)
-        nc.sync.dma_start(out=range_rows[:], in_=w_range.rearrange("(b i) -> b i", i=32).partition_broadcast(4))
         load_rows(r_raw[0][0], err, 0, 0)
+        nc.sync.dma_start(out=range_rows[:], in_=w_range.rearrange("(b i) -> b i", i=32).partition_broadcast(4))
         load_a(2, slice(0, DI))
-        load_q(2, 0)
         load_rows(r_raw[1][0], err, 1, 0)
+        load_q(2, 0)
         load_rows(r_raw[2][0], err, 2, 0)
         load_rows(mag[0][0], w_mag, 0, 0)
+        load_scales(q_sc[1], err8_scales, Q_ROW, half(1), range(0, 2))
         load_rows(mag[1][0], w_mag, 1, 0)
-        load_scales(q_sc[1], err8_scales, Q_ROW, half(1))
-        load_scales(p_sc[1], err4_scales, 0, half(1))
+        load_scales(q_sc[1], err8_scales, Q_ROW, half(1), range(2, 4))
         load_q_all(1)
+        load_scales(p_sc[1], err4_scales, 0, half(1), range(0, 2))
         load_p(1)
+        load_scales(p_sc[1], err4_scales, 0, half(1), range(2, 4))
         for g in range(G):
             load_rows(r_raw[g][1], err, g, 1)
         load_rows(mag[0][1], w_mag, 0, 1)
@@ -238,15 +246,23 @@ def tile_straight_through_weight_grad_k3_kernel(
         order_a_scales(0, 0)
         order_a_scales(0, 1)
         order_a_codes(0, 1)
-        for g in (1, 2):
-            order_a_scales(g, 0)
-            order_a_scales(g, 1)
-            order_a_codes(g, 0)
-            order_a_codes(g, 1)
-            if g == 1:
-                nc.vector.transpose(out=range_cols[:], in_=range_rows[:])
-                nc.scalar.copy(out=range_wide[:], in_=range_cols[:].unsqueeze(2).to_broadcast([P, 32, 32]))
+        order_a_codes(1, 0)
+        order_a_scales(1, 0)
+        order_a_scales(1, 1)
+        order_a_codes(1, 1)
+        order_a_scales(2, 0)
+        order_a_scales(2, 1)
+        grouped = [interleave(nc.scalar.copy, r_raw[0][0][:], HALF)]
+        nc.vector.transpose(out=range_cols[:], in_=range_rows[:])
+        nc.vector.tensor_copy(out=range_wide[:], in_=range_cols[:].unsqueeze(2).to_broadcast([P, 32, 32]))
+        order_a_codes(2, 0)
+        order_a_codes(2, 1)
         nc.vector.transpose(out=range_all[:], in_=range_wide[:].rearrange("p b j -> p (b j)"))
+
+        warm(WARM_FIRST, warm_codes[:], warm_sc[:], warm_codes[:])
+        warm(WARM_NEXT, a_codes[0][0][:, :P], warm_sc[:], warm_codes[:])
+        warm(WARM_NEXT, a_codes[0][0][:, :P], a_sc[0][0][:, :P], warm_codes[:])
+        warm(WARM_NEXT, a_codes[0][0][:, :P], a_sc[0][0][:, :P], q_codes[0][:, 0, :P])
 
         acc = [[new_acc(HALF) for t in range(PACK)] for m in range(2)]
         for g in range(G):
@@ -255,11 +271,12 @@ def tile_straight_through_weight_grad_k3_kernel(
                     for t in range(PACK):
                         one_pass(acc[m][t], g, m, 0, t, full)
 
-        grouped = [interleave(nc.scalar.copy, r_raw[g][0][:], HALF) for g in range(G)]
+        grouped.append(interleave(nc.scalar.copy, r_raw[1][0][:], HALF))
         quantize_r(0, 0, grouped[0])
+        grouped.append(interleave(nc.vector.tensor_copy, r_raw[2][0][:], HALF))
         quantize_r(1, 0, grouped[1])
-        make_mask(0, 0)
         quantize_r(2, 0, grouped[2])
+        make_mask(0, 0)
         make_mask(1, 0)
 
         for g in range(G):
@@ -269,7 +286,7 @@ def tile_straight_through_weight_grad_k3_kernel(
             for g in range(G):
                 pass_r(acc[1][t], g, 1, 0, t, full)
 
-        grouped = [interleave(nc.scalar.copy, r_raw[g][1][:], HALF) for g in range(G)]
+        grouped = [interleave(nc.scalar.copy, r_raw[g][1][:], HALF) for g in range(2)]
         for t in range(PACK):
             apply_mask(acc[0][t], 0, 0, t, full)
         store_y(0, 0, all_t, full)
@@ -280,8 +297,9 @@ def tile_straight_through_weight_grad_k3_kernel(
         apply_mask(acc[1][2], 1, 0, 2, full)
         apply_mask(acc[1][3], 1, 0, 3, full)
         store_y(1, 0, all_t, full)
-        quantize_r(2, 1, grouped[2])
+        grouped.append(interleave(nc.vector.tensor_copy, r_raw[2][1][:], HALF))
         make_mask(0, 1)
+        quantize_r(2, 1, grouped[2])
 
         acc = [new_acc(HALF) for t in range(PACK)]
         for t in range(PACK):

@@ -30,12 +30,12 @@ def tile_straight_through_weight_grad_k3_kernel(
     nc = tc.nc
     with ExitStack() as ctx:
         keep = ctx.enter_context(tc.tile_pool(name="keep", bufs=1))
-        stage = ctx.enter_context(tc.tile_pool(name="stage", bufs=3))
+        stage = ctx.enter_context(tc.tile_pool(name="stage", bufs=4))
         psum = ctx.enter_context(tc.psum_pool(name="psum", bufs=1))
         ctx.enter_context(tc.manual_schedule())
 
         def kept(name, shape, dtype):
-            return keep.tile(shape, dtype, name=name, align_bytes=64)
+            return keep.tile(shape, dtype, name=name, align_bytes=256)
 
         a_raw = [kept("a_raw%d" % g, [P, DI], U32) for g in range(G)]
         a_codes = [[kept("a_codes%d%d" % (g, m), [P, HALF], U32) for m in range(2)] for g in range(G)]
@@ -76,9 +76,9 @@ def tile_straight_through_weight_grad_k3_kernel(
             src = err8_words.rearrange("g p n t -> p g (n t)").bitcast(I32)
             nc.sync.dma_start(out=q_codes[h][:].bitcast(I32), in_=src[:, :, half(h)])
 
-        def load_p(h):
-            src = err4_words.rearrange("g p b -> p g b")[:, :, 2 * HALF * h : 2 * HALF * (h + 1)]
-            nc.sync.dma_start(out=p_codes[h][:].bitcast(I32), in_=src.bitcast(I32))
+        def load_p(gs, h):
+            src = err4_words.rearrange("g p b -> p g b")[:, gs, 2 * HALF * h : 2 * HALF * (h + 1)]
+            nc.sync.dma_start(out=p_codes[h][:, gs, :].bitcast(I32), in_=src.bitcast(I32))
 
         def load_scales(plane, dram, first_row, cols, rows=range(4)):
             src = dram.rearrange("g (q r) n -> r q g n", r=4)
@@ -104,7 +104,7 @@ def tile_straight_through_weight_grad_k3_kernel(
             )
 
         def interleave(copy, src, width):
-            grouped = stage.tile([P, HALF * PACK], BF16, name="grouped", align_bytes=64)
+            grouped = stage.tile([P, HALF * PACK], BF16, name="grouped", align_bytes=256)
             copy(
                 out=grouped[:, : width * PACK].rearrange("p (c i t) -> p c t i", i=4, t=PACK),
                 in_=src.rearrange("p t (c i) -> p c t i", i=4),
@@ -219,23 +219,24 @@ def tile_straight_through_weight_grad_k3_kernel(
         load_scales(q_sc[0], err8_scales, Q_ROW, half(0), range(2, 4))
         load_a(0, half(1))
         load_scales(p_sc[0], err4_scales, 0, half(0))
-        load_p(0)
-        load_a(1, slice(0, DI))
+        load_p(slice(0, 1), 0)
+        load_a(1, half(0))
         load_scales(a_sc_rest, a_scales[1:G], 0, slice(0, DI))
         load_q(1, 0)
-        load_rows(r_raw[0][0], err, 0, 0)
-        nc.sync.dma_start(out=range_rows[:], in_=w_range.rearrange("(b i) -> b i", i=32).partition_broadcast(4))
+        load_a(1, half(1))
+        load_p(slice(1, G), 0)
         load_a(2, slice(0, DI))
-        load_rows(r_raw[1][0], err, 1, 0)
         load_q(2, 0)
-        load_rows(r_raw[2][0], err, 2, 0)
+        nc.sync.dma_start(out=range_rows[:], in_=w_range.rearrange("(b i) -> b i", i=32).partition_broadcast(4))
+        for g in range(G):
+            load_rows(r_raw[g][0], err, g, 0)
         load_rows(mag[0][0], w_mag, 0, 0)
         load_scales(q_sc[1], err8_scales, Q_ROW, half(1), range(0, 2))
         load_rows(mag[1][0], w_mag, 1, 0)
         load_scales(q_sc[1], err8_scales, Q_ROW, half(1), range(2, 4))
         load_q_all(1)
         load_scales(p_sc[1], err4_scales, 0, half(1), range(0, 2))
-        load_p(1)
+        load_p(slice(0, G), 1)
         load_scales(p_sc[1], err4_scales, 0, half(1), range(2, 4))
         for g in range(G):
             load_rows(r_raw[g][1], err, g, 1)
@@ -252,11 +253,10 @@ def tile_straight_through_weight_grad_k3_kernel(
         order_a_codes(1, 1)
         order_a_scales(2, 0)
         order_a_scales(2, 1)
-        grouped = [interleave(nc.scalar.copy, r_raw[0][0][:], HALF)]
-        nc.vector.transpose(out=range_cols[:], in_=range_rows[:])
-        nc.vector.tensor_copy(out=range_wide[:], in_=range_cols[:].unsqueeze(2).to_broadcast([P, 32, 32]))
         order_a_codes(2, 0)
         order_a_codes(2, 1)
+        nc.vector.transpose(out=range_cols[:], in_=range_rows[:])
+        nc.vector.tensor_copy(out=range_wide[:], in_=range_cols[:].unsqueeze(2).to_broadcast([P, 32, 32]))
         nc.vector.transpose(out=range_all[:], in_=range_wide[:].rearrange("p b j -> p (b j)"))
 
         warm(WARM_FIRST, warm_codes[:], warm_sc[:], warm_codes[:])
@@ -271,51 +271,48 @@ def tile_straight_through_weight_grad_k3_kernel(
                     for t in range(PACK):
                         one_pass(acc[m][t], g, m, 0, t, full)
 
-        grouped.append(interleave(nc.scalar.copy, r_raw[1][0][:], HALF))
-        quantize_r(0, 0, grouped[0])
-        grouped.append(interleave(nc.vector.tensor_copy, r_raw[2][0][:], HALF))
-        quantize_r(1, 0, grouped[1])
-        quantize_r(2, 0, grouped[2])
+        r0 = interleave(nc.scalar.copy, r_raw[0][0][:], HALF)
+        r1 = interleave(nc.vector.tensor_copy, r_raw[1][0][:], HALF)
+        r2 = interleave(nc.scalar.copy, r_raw[2][0][:], HALF)
+        quantize_r(0, 0, r0)
+        quantize_r(1, 0, r1)
         make_mask(0, 0)
+        quantize_r(2, 0, r2)
         make_mask(1, 0)
 
         for g in range(G):
-            for t in range(PACK):
-                pass_r(acc[0][t], g, 0, 0, t, full)
-        for t in range(PACK):
-            for g in range(G):
-                pass_r(acc[1][t], g, 1, 0, t, full)
+            for m in range(2):
+                for t in range(PACK):
+                    pass_r(acc[m][t], g, m, 0, t, full)
 
-        grouped = [interleave(nc.scalar.copy, r_raw[g][1][:], HALF) for g in range(2)]
-        for t in range(PACK):
-            apply_mask(acc[0][t], 0, 0, t, full)
-        store_y(0, 0, all_t, full)
-        quantize_r(0, 1, grouped[0])
-        apply_mask(acc[1][0], 1, 0, 0, full)
-        apply_mask(acc[1][1], 1, 0, 1, full)
-        quantize_r(1, 1, grouped[1])
-        apply_mask(acc[1][2], 1, 0, 2, full)
-        apply_mask(acc[1][3], 1, 0, 3, full)
-        store_y(1, 0, all_t, full)
-        grouped.append(interleave(nc.vector.tensor_copy, r_raw[2][1][:], HALF))
+        r0 = interleave(nc.scalar.copy, r_raw[0][1][:], HALF)
+        r2 = interleave(nc.scalar.copy, r_raw[2][1][:], HALF)
+        for m in range(2):
+            for t in range(PACK):
+                apply_mask(acc[m][t], m, 0, t, full)
+            store_y(m, 0, all_t, full)
+        r1 = interleave(nc.vector.tensor_copy, r_raw[1][1][:], HALF)
+        quantize_r(0, 1, r0)
+        y0 = interleave(nc.vector.tensor_copy, y[0][0][:], HALF)
+        quantize_r(1, 1, r1)
+        quantize_y(0, 0, full, y0)
+        store_codes(0, 0, full)
+        quantize_r(2, 1, r2)
+        y1 = interleave(nc.scalar.copy, y[1][0][:], HALF)
         make_mask(0, 1)
-        quantize_r(2, 1, grouped[2])
+        make_mask(1, 1)
+        quantize_y(1, 0, full, y1)
+        store_codes(1, 0, full)
+        store_scales(slice(0, 2), 0, [nc.sync] * 4)
 
         acc = [new_acc(HALF) for t in range(PACK)]
         for t in range(PACK):
             for one_pass in (pass_q, pass_p):
                 for g in range(G):
                     one_pass(acc[t], g, 0, 1, t, full)
-        for t in range(PACK):
-            for g in range(G):
+        for g in range(G):
+            for t in range(PACK):
                 pass_r(acc[t], g, 0, 1, t, full)
-
-        quantize_y(0, 0, full, interleave(nc.scalar.copy, y[0][0][:], HALF))
-        store_codes(0, 0, full)
-        make_mask(1, 1)
-        quantize_y(1, 0, full, interleave(nc.scalar.copy, y[1][0][:], HALF))
-        store_codes(1, 0, full)
-        store_scales(slice(0, 2), 0, [nc.sync] * 4)
 
         for t in range(PACK):
             apply_mask(acc[t], 0, 1, t, full)
@@ -328,7 +325,7 @@ def tile_straight_through_weight_grad_k3_kernel(
             lo += width
             last = lo == HALF
             if last:
-                final = stage.tile([P, HALF * PACK], BF16, name="grouped", align_bytes=64)
+                final = stage.tile([P, HALF * PACK], BF16, name="grouped", align_bytes=256)
                 final = final[:, : width * PACK]
                 by_t = final.rearrange("p (c t) -> p c t", t=PACK)
             for t in range(PACK):
@@ -336,16 +333,16 @@ def tile_straight_through_weight_grad_k3_kernel(
                 for one_pass in (pass_q, pass_p, pass_r):
                     for g in range(G):
                         one_pass(acc, g, 1, 1, t, cols)
-                if t == PACK - 2:
+                if last and t >= 2:
+                    nc.vector.tensor_tensor(out=by_t[:, :, t], in0=acc, in1=mask[1][1][:, t, cols], op=ALU.mult)
+                apply_mask(acc, 1, 1, t, cols)
+                if t == (PACK - 1 if pending[0] == 0 else 1):
                     quantize_y(pending[0], 1, pending[1], pending[2])
                     store_codes(pending[0], 1, pending[1])
                     if pending[0] == 0:
                         store_scales(slice(0, 1), 1, [nc.sync] * 4)
-                if last and t >= 2:
-                    nc.vector.tensor_tensor(out=by_t[:, :, t], in0=acc, in1=mask[1][1][:, t, cols], op=ALU.mult)
-                apply_mask(acc, 1, 1, t, cols)
                 if last and t == 1:
-                    nc.scalar.copy(out=by_t[:, :, 0:2], in_=y[1][1][:, 0:2, cols].rearrange("p t c -> p c t"))
+                    nc.vector.tensor_copy(out=by_t[:, :, 0:2], in_=y[1][1][:, 0:2, cols].rearrange("p t c -> p c t"))
                 if last and t == PACK - 2:
                     store_y(1, 1, slice(0, PACK - 1), cols)
             if last:

from contextlib import ExitStack

import concourse.mybir as mybir

T, DI, DO = 1536, 1024, 1024
FLOPS = 3 * 2 * T * DI * DO

F32 = mybir.dt.float32
BF16 = mybir.dt.bfloat16
I32 = mybir.dt.int32
U32 = mybir.dt.uint32
U8 = mybir.dt.uint8
FP8X4 = mybir.dt.float8_e4m3fn_x4
FP4X4 = mybir.dt.float4_e2m1fn_x4
ALU = mybir.AluOpType

P = 128
PACK = 4
GROUP = P * PACK
G = T // GROUP
HALF = 512
Q_ROW = 4
LAST_CHUNKS = (256, 128, 128)
WARM_FIRST, WARM_NEXT = 10, 4


def tile_straight_through_weight_grad_k3_kernel(
    tc, a_words, a_scales, err4_words, err4_scales, err8_words, err8_scales, err, w_mag, w_range, out_0, out_1, out_2
):
    nc = tc.nc
    with ExitStack() as ctx:
        keep = ctx.enter_context(tc.tile_pool(name="keep", bufs=1))
        stage = ctx.enter_context(tc.tile_pool(name="stage", bufs=4))
        psum = ctx.enter_context(tc.psum_pool(name="psum", bufs=1))
        ctx.enter_context(tc.manual_schedule())

        def kept(name, shape, dtype):
            return keep.tile(shape, dtype, name=name, align_bytes=256)

        a_raw = [kept("a_raw%d" % g, [P, DI], U32) for g in range(G)]
        a_codes = [[kept("a_codes%d%d" % (g, m), [P, HALF], U32) for m in range(2)] for g in range(G)]
        a_sc_first = kept("a_sc_first", [P, 1, DI], U8)
        a_sc_rest = kept("a_sc_rest", [P, G - 1, DI], U8)
        a_sc_raw = [a_sc_first[:, 0, :], a_sc_rest[:, 0, :], a_sc_rest[:, 1, :]]
        a_sc = [[kept("a_sc%d%d" % (g, m), [P, HALF], U8) for m in range(2)] for g in range(G)]
        q_codes = [kept("q_codes%d" % h, [P, G, HALF], U32) for h in range(2)]
        q_sc = [kept("q_sc%d" % h, [P, G, HALF], U8) for h in range(2)]
        p_codes = [kept("p_codes%d" % h, [P, G, 2 * HALF], U8) for h in range(2)]
        p_sc = [kept("p_sc%d" % h, [P, G, HALF], U8) for h in range(2)]
        r_raw = [[kept("r_raw%d%d" % (g, h), [P, PACK, HALF], BF16) for h in range(2)] for g in range(G)]
        r_codes = [[kept("r_codes%d%d" % (g, h), [P, HALF], U32) for h in range(2)] for g in range(G)]
        r_sc = [[kept("r_sc%d%d" % (g, h), [P, HALF], U8) for h in range(2)] for g in range(G)]
        mag = [[kept("mag%d%d" % (m, h), [P, PACK, HALF], BF16) for h in range(2)] for m in range(2)]
        mask = [[kept("mask%d%d" % (m, h), [P, PACK, HALF], BF16) for h in range(2)] for m in range(2)]
        y = [[kept("y%d%d" % (m, h), [P, PACK, HALF], F32) for h in range(2)] for m in range(2)]
        y_codes = [[kept("y_codes%d%d" % (m, h), [P, HALF], U32) for h in range(2)] for m in range(2)]
        y_sc = kept("y_sc", [P, 2, DO], U8)
        range_rows = kept("range_rows", [P, 32], BF16)
        range_cols = kept("range_cols", [P, 32], BF16)
        range_wide = kept("range_wide", [P, 32, 32], BF16)
        range_all = kept("range_all", [P, DO], BF16)

        def half(h):
            return slice(h * HALF, (h + 1) * HALF)

        def words_of(dram, g):
            return dram[g].rearrange("p n t -> p (n t)").bitcast(I32)

        def load_a(g, cols):
            nc.sync.dma_start(out=a_raw[g][:, cols].bitcast(I32), in_=words_of(a_words, g)[:, cols])

        def load_q(g, h):
            nc.sync.dma_start(out=q_codes[h][:, g, :].bitcast(I32), in_=words_of(err8_words, g)[:, half(h)])

        def load_q_all(h):
            src = err8_words.rearrange("g p n t -> p g (n t)").bitcast(I32)
            nc.sync.dma_start(out=q_codes[h][:].bitcast(I32), in_=src[:, :, half(h)])

        def load_p(gs, h):
            src = err4_words.rearrange("g p b -> p g b")[:, gs, 2 * HALF * h : 2 * HALF * (h + 1)]
            nc.sync.dma_start(out=p_codes[h][:, gs, :].bitcast(I32), in_=src.bitcast(I32))

        def load_scales(plane, dram, first_row, cols, rows=range(4)):
            src = dram.rearrange("g (q r) n -> r q g n", r=4)
            for r in rows:
                nc.sync.dma_start(
                    out=plane[first_row + r : P : 32, :, :].bitcast(I32), in_=src[r][:, :, cols].bitcast(I32)
                )

        def load_rows(tile, dram, g, h):
            src = dram[g * GROUP : (g + 1) * GROUP, :].rearrange("(p t) n -> p t n", t=PACK)
            nc.sync.dma_start(out=tile[:], in_=src[:, :, half(h)])

        def order_a_codes(g, m):
            nc.vector.tensor_copy(
                out=a_codes[g][m][:].bitcast(I32).rearrange("p (t c) -> p c t", t=PACK),
                in_=a_raw[g][:, half(m)].bitcast(I32).rearrange("p (c t) -> p c t", t=PACK),
            )

        def order_a_scales(g, m):
            nc.vector.tensor_copy(
                out=a_sc[g][m][:].rearrange("p (t c) -> p t c", t=PACK),
                in_=a_sc_raw[g][:, half(m)].rearrange("p (c t) -> p t c", t=PACK),
            )

        def interleave(copy, src, width):
            grouped = stage.tile([P, HALF * PACK], BF16, name="grouped", align_bytes=256)
            copy(
                out=grouped[:, : width * PACK].rearrange("p (c i t) -> p c t i", i=4, t=PACK),
                in_=src.rearrange("p t (c i) -> p c t i", i=4),
            )
            return grouped[:, : width * PACK]

        def quantize_r(g, h, grouped):
            nc.vector.quantize_mx(out=r_codes[g][h][:].bitcast(FP8X4), scales=r_sc[g][h][:], in_=grouped)

        def quantize_y(m, h, cols, grouped):
            whole = slice(h * HALF + cols.start, h * HALF + cols.stop)
            nc.vector.quantize_mx(out=y_codes[m][h][:, cols].bitcast(FP8X4), scales=y_sc[:, m, whole], in_=grouped)

        def make_mask(m, h):
            nc.vector.tensor_tensor(
                out=mask[m][h][:],
                in0=mag[m][h][:],
                in1=range_all[:, half(h)].unsqueeze(1).to_broadcast([P, PACK, HALF]),
                op=ALU.is_le,
            )

        def apply_mask(acc, m, h, t, cols):
            nc.vector.tensor_tensor(out=y[m][h][:, t, cols], in0=acc, in1=mask[m][h][:, t, cols], op=ALU.mult)

        banks_used = []

        def new_acc(width):
            bank = len(banks_used) % 8
            banks_used.append(bank)
            acc = psum.tile([P, HALF], F32, name="acc%d" % bank)
            return acc[:, :width]

        def mx(acc, g, m, t, codes, scales, start=False, stop=False):
            mine = slice(t * P, (t + 1) * P)
            nc.tensor.matmul_mx(
                out=acc,
                lhsT=a_codes[g][m][:, mine].bitcast(FP8X4),
                lhsT_scale=a_sc[g][m][:, mine],
                rhs=codes,
                rhs_scale=scales,
                start=start,
                stop=stop,
            )

        def pass_q(acc, g, m, h, t, cols):
            mx(acc, g, m, t, q_codes[h][:, g, cols].bitcast(FP8X4), q_sc[h][Q_ROW:P, g, cols], start=(g == 0))

        def pass_p(acc, g, m, h, t, cols):
            width = cols.stop - cols.start
            step = width if width == HALF else P
            for c in range(0, width, step):
                lo = cols.start + c
                codes = p_codes[h][:, g, 2 * lo : 2 * (lo + step)].bitcast(FP4X4)
                mx(acc[:, c : c + step], g, m, t, codes, p_sc[h][:, g, lo : lo + step])

        def pass_r(acc, g, m, h, t, cols):
            mx(acc, g, m, t, r_codes[g][h][:, cols].bitcast(FP8X4), r_sc[g][h][:, cols], stop=(g == G - 1))

        def store_y(m, h, ts, cols):
            dst = out_0[m * GROUP : (m + 1) * GROUP, :].rearrange("(p t) n -> p t n", t=PACK)
            nc.sync.dma_start(out=dst[:, ts, h * HALF + cols.start : h * HALF + cols.stop], in_=y[m][h][:, ts, cols])

        def store_codes(m, h, cols):
            dst = out_1[m].rearrange("p n t -> p (n t)").bitcast(I32)
            nc.sync.dma_start(
                out=dst[:, h * HALF + cols.start : h * HALF + cols.stop], in_=y_codes[m][h][:, cols].bitcast(I32)
            )

        def store_scales(ms, h, queues):
            dst = out_2.rearrange("m q n -> q m n")
            for q in range(4):
                queues[q].dma_start(
                    out=dst[4 * q : 4 * q + 4, ms, half(h)].bitcast(I32),
                    in_=y_sc[32 * q : 32 * q + 4, ms, half(h)].bitcast(I32),
                )

        full = slice(0, HALF)
        all_t = slice(0, PACK)

        def clear(plane):
            nc.vector.memset(plane[:].rearrange("p g n -> p (g n)").bitcast(I32), 0)

        warm_in = kept("warm_in", [P, P * PACK], BF16)
        warm_codes = kept("warm_codes", [P, P], U32)
        warm_sc = kept("warm_sc", [P, P], U8)
        clear(a_sc_first)
        clear(q_sc[0])
        nc.vector.memset(warm_in[:], 1.0)
        clear(p_sc[0])
        nc.vector.quantize_mx(out=warm_codes[:].bitcast(FP8X4), scales=warm_sc[:], in_=warm_in[:])
        clear(a_sc_rest)
        clear(q_sc[1])
        clear(p_sc[1])
        warm_acc = psum.tile([P, HALF], F32, name="acc7")

        def warm(count, lhs, lhs_scales, rhs):
            for i in range(count):
                nc.tensor.matmul_mx(
                    out=warm_acc[:, :P],
                    lhsT=lhs.bitcast(FP8X4),
                    lhsT_scale=lhs_scales,
                    rhs=rhs.bitcast(FP8X4),
                    rhs_scale=warm_sc[:],
                    start=True,
                    stop=True,
                )

        load_a(0, half(0))
        load_scales(a_sc_first, a_scales[0:1], 0, slice(0, DI))
        load_scales(q_sc[0], err8_scales, Q_ROW, half(0), range(0, 2))
        load_q(0, 0)
        load_scales(q_sc[0], err8_scales, Q_ROW, half(0), range(2, 4))
        load_a(0, half(1))
        load_scales(p_sc[0], err4_scales, 0, half(0))
        load_p(slice(0, 1), 0)
        load_a(1, half(0))
        load_scales(a_sc_rest, a_scales[1:G], 0, slice(0, DI))
        load_q(1, 0)
        load_a(1, half(1))
        load_p(slice(1, G), 0)
        load_a(2, slice(0, DI))
        load_q(2, 0)
        nc.sync.dma_start(out=range_rows[:], in_=w_range.rearrange("(b i) -> b i", i=32).partition_broadcast(4))
        for g in range(G):
            load_rows(r_raw[g][0], err, g, 0)
        load_rows(mag[0][0], w_mag, 0, 0)
        load_scales(q_sc[1], err8_scales, Q_ROW, half(1), range(0, 2))
        load_rows(mag[1][0], w_mag, 1, 0)
        load_scales(q_sc[1], err8_scales, Q_ROW, half(1), range(2, 4))
        load_q_all(1)
        load_scales(p_sc[1], err4_scales, 0, half(1), range(0, 2))
        load_p(slice(0, G), 1)
        load_scales(p_sc[1], err4_scales, 0, half(1), range(2, 4))
        for g in range(G):
            load_rows(r_raw[g][1], err, g, 1)
        load_rows(mag[0][1], w_mag, 0, 1)
        load_rows(mag[1][1], w_mag, 1, 1)

        order_a_codes(0, 0)
        order_a_scales(0, 0)
        order_a_scales(0, 1)
        order_a_codes(0, 1)
        order_a_codes(1, 0)
        order_a_scales(1, 0)
        order_a_scales(1, 1)
        order_a_codes(1, 1)
        order_a_scales(2, 0)
        order_a_scales(2, 1)
        order_a_codes(2, 0)
        order_a_codes(2, 1)
        nc.vector.transpose(out=range_cols[:], in_=range_rows[:])
        nc.vector.tensor_copy(out=range_wide[:], in_=range_cols[:].unsqueeze(2).to_broadcast([P, 32, 32]))
        nc.vector.transpose(out=range_all[:], in_=range_wide[:].rearrange("p b j -> p (b j)"))

        warm(WARM_FIRST, warm_codes[:], warm_sc[:], warm_codes[:])
        warm(WARM_NEXT, a_codes[0][0][:, :P], warm_sc[:], warm_codes[:])
        warm(WARM_NEXT, a_codes[0][0][:, :P], a_sc[0][0][:, :P], warm_codes[:])
        warm(WARM_NEXT, a_codes[0][0][:, :P], a_sc[0][0][:, :P], q_codes[0][:, 0, :P])

        acc = [[new_acc(HALF) for t in range(PACK)] for m in range(2)]
        for g in range(G):
            for one_pass in (pass_q, pass_p):
                for m in range(2):
                    for t in range(PACK):
                        one_pass(acc[m][t], g, m, 0, t, full)

        r0 = interleave(nc.scalar.copy, r_raw[0][0][:], HALF)
        r1 = interleave(nc.vector.tensor_copy, r_raw[1][0][:], HALF)
        r2 = interleave(nc.scalar.copy, r_raw[2][0][:], HALF)
        quantize_r(0, 0, r0)
        quantize_r(1, 0, r1)
        make_mask(0, 0)
        quantize_r(2, 0, r2)
        make_mask(1, 0)

        for g in range(G):
            for m in range(2):
                for t in range(PACK):
                    pass_r(acc[m][t], g, m, 0, t, full)

        r0 = interleave(nc.scalar.copy, r_raw[0][1][:], HALF)
        r2 = interleave(nc.scalar.copy, r_raw[2][1][:], HALF)
        for m in range(2):
            for t in range(PACK):
                apply_mask(acc[m][t], m, 0, t, full)
            store_y(m, 0, all_t, full)
        r1 = interleave(nc.vector.tensor_copy, r_raw[1][1][:], HALF)
        quantize_r(0, 1, r0)
        y0 = interleave(nc.vector.tensor_copy, y[0][0][:], HALF)
        quantize_r(1, 1, r1)
        quantize_y(0, 0, full, y0)
        store_codes(0, 0, full)
        quantize_r(2, 1, r2)
        y1 = interleave(nc.scalar.copy, y[1][0][:], HALF)
        make_mask(0, 1)
        make_mask(1, 1)
        quantize_y(1, 0, full, y1)
        store_codes(1, 0, full)
        store_scales(slice(0, 2), 0, [nc.sync] * 4)

        acc = [new_acc(HALF) for t in range(PACK)]
        for t in range(PACK):
            for one_pass in (pass_q, pass_p):
                for g in range(G):
                    one_pass(acc[t], g, 0, 1, t, full)
        for g in range(G):
            for t in range(PACK):
                pass_r(acc[t], g, 0, 1, t, full)

        for t in range(PACK):
            apply_mask(acc[t], 0, 1, t, full)
        store_y(0, 1, all_t, full)
        pending = (0, full, interleave(nc.scalar.copy, y[0][1][:], HALF))

        lo = 0
        for width in LAST_CHUNKS:
            cols = slice(lo, lo + width)
            lo += width
            last = lo == HALF
            if last:
                final = stage.tile([P, HALF * PACK], BF16, name="grouped", align_bytes=256)
                final = final[:, : width * PACK]
                by_t = final.rearrange("p (c t) -> p c t", t=PACK)
            for t in range(PACK):
                acc = new_acc(width)
                for one_pass in (pass_q, pass_p, pass_r):
                    for g in range(G):
                        one_pass(acc, g, 1, 1, t, cols)
                if last and t >= 2:
                    nc.vector.tensor_tensor(out=by_t[:, :, t], in0=acc, in1=mask[1][1][:, t, cols], op=ALU.mult)
                apply_mask(acc, 1, 1, t, cols)
                if t == (PACK - 1 if pending[0] == 0 else 1):
                    quantize_y(pending[0], 1, pending[1], pending[2])
                    store_codes(pending[0], 1, pending[1])
                    if pending[0] == 0:
                        store_scales(slice(0, 1), 1, [nc.sync] * 4)
                if last and t == 1:
                    nc.vector.tensor_copy(out=by_t[:, :, 0:2], in_=y[1][1][:, 0:2, cols].rearrange("p t c -> p c t"))
                if last and t == PACK - 2:
                    store_y(1, 1, slice(0, PACK - 1), cols)
            if last:
                store_y(1, 1, slice(PACK - 1, PACK), cols)
                quantize_y(1, 1, cols, final)
                store_codes(1, 1, cols)
                store_scales(slice(1, 2), 1, [nc.sync] * 4)
            else:
                store_y(1, 1, all_t, cols)
                pending = (1, cols, interleave(nc.scalar.copy, y[1][1][:, :, cols], width))
